import numpy as np
import ml_dtypes


def mxq(x, axis, fmt="e4m3"):
    dtype, down = {"e4m3": (ml_dtypes.float8_e4m3fn, 7), "e5m2": (ml_dtypes.float8_e5m2, 14)}[fmt]
    v = np.moveaxis(np.asarray(x, np.float32).astype(ml_dtypes.bfloat16).astype(np.float64), axis, -1)
    blocks = v.reshape(v.shape[:-1] + (-1, 32))
    amax = np.abs(blocks).max(-1, keepdims=True)
    byte = np.maximum(np.where(amax > 0, np.frexp(amax)[1] - 1 + 127, 0) - down, 1)
    scale = np.exp2(byte - 127.0)
    codes = (blocks / scale).astype(np.float32).astype(dtype).astype(np.float64)
    return np.moveaxis((codes * scale).reshape(v.shape), -1, axis)


WIDE = False


def mx_kscale(k):
    if not WIDE:
        return np.ones(k)
    levels = np.array([10, -10, 5, -5, 0])
    if k % 512:
        return np.exp2(np.random.permutation(np.resize(levels, k // 32))).repeat(32)
    a = np.empty((k // 512, 16))
    for p in range(k // 512):
        a[p, :8] = np.random.permutation(np.resize(levels, 8))
        for g in range(8):
            far = levels[np.abs(levels - a[p, g]) >= 10]
            a[p, g + 8] = far[np.random.randint(len(far))]
    return np.exp2(a.ravel()).repeat(32)


BF16 = ml_dtypes.bfloat16


def bf(x):
    return np.asarray(x, np.float32).astype(BF16)


def f64(x):
    return np.asarray(x).astype(np.float64)


E2M1 = np.array([0.0, 0.5, 1.0, 1.5, 2.0, 3.0, 4.0, 6.0, -0.0, -0.5, -1.0, -1.5, -2.0, -3.0, -4.0, -6.0])


def pack_weight(w, fmt):
    k, n = w.shape
    w = f64(bf(w)).reshape(k // 32, 32, n)
    amax = np.abs(w).max(1)
    if fmt == "e4m3":
        byte = np.frexp(amax)[1] - 1 + 127 - 7
    else:
        mant, ex = np.frexp(amax / 6.0)
        byte = np.where(mant > 0.5, ex, ex - 1) + 127
    byte = np.clip(np.where(amax > 0, byte, 1), 1, 254)
    scaled = (w * np.exp2(127.0 - byte)[:, None, :]).reshape(k, n).astype(np.float32)
    by_word = np.ascontiguousarray(scaled.reshape(k // 512, 128, 4, n).transpose(0, 1, 3, 2))
    if fmt == "e4m3":
        words = by_word.astype(ml_dtypes.float8_e4m3fn).view(np.uint8)
    else:
        c = by_word.astype(ml_dtypes.float4_e2m1fn).view(np.uint8) & 0xF
        words = c[..., 0::2] | (c[..., 1::2] << 4)
    return np.ascontiguousarray(words), np.ascontiguousarray(byte.astype(np.uint8).reshape(k // 512, 16, n))


def unpack_weight(words, scales, fmt):
    g, p, n, _ = words.shape
    if fmt == "e4m3":
        vals = np.ascontiguousarray(words).view(ml_dtypes.float8_e4m3fn).astype(np.float64)
    else:
        nib = np.empty((g, p, n, 4), np.uint8)
        nib[..., 0::2] = words & 0xF
        nib[..., 1::2] = words >> 4
        vals = E2M1[nib]
    vals = vals * np.repeat(np.exp2(scales.astype(np.float64) - 127.0), 8, axis=1)[..., None]
    return vals.transpose(0, 1, 3, 2).reshape(g * 512, n)
def pack4(w):
    words, scales = pack_weight(w, "e2m1")
    return words.reshape(words.shape[0], 128, -1), scales


def unpack4(words, scales):
    return unpack_weight(words.reshape(words.shape[0], 128, -1, 2), scales, "e2m1")


def planes(Y):
    n, m = Y.shape
    b = f64(bf(Y)).reshape(n // 32, 32, m)
    amax = np.abs(b).max(1)
    byte = np.clip(np.where(amax > 0, np.frexp(amax)[1] - 1 + 127 - 7, 1), 1, 254)
    codes = (b * np.exp2(127.0 - byte)[:, None, :]).reshape(n, m).astype(np.float32).astype(ml_dtypes.float8_e4m3fn).view(np.uint8)
    words = codes.reshape(n // 512, 128, 4, m).transpose(0, 1, 3, 2)
    return np.ascontiguousarray(words), np.ascontiguousarray(byte.astype(np.uint8).reshape(n // 512, 16, m))


B, K, N = 768, 1536, 1024
SPREAD = 1.5
AMP = np.sqrt(K / np.exp(SPREAD ** 2))


def setup_inputs():
    s = mx_kscale(K)
    cost = SPREAD * np.random.randn(B, K)
    w = np.exp(-(cost - cost.min(axis=1, keepdims=True)))
    w = w / w.sum(axis=1, keepdims=True)
    sigma = 0.8 * np.exp(0.8 * np.random.randn(N))
    noise = AMP * np.random.randn(K, N) * sigma
    offset = 0.6 * AMP * np.random.randn(K, N) * sigma
    gate = AMP * np.random.randn(K, N)
    x_words, x_scales = pack_weight(w.T * s[:, None], "e4m3")
    e_words, e_scales = pack4(noise / s[:, None])
    f_words, f_scales = pack_weight(offset / s[:, None], "e4m3")
    return {"x_words": x_words, "x_scales": x_scales,
            "e_words": e_words, "e_scales": e_scales,
            "f_words": f_words, "f_scales": f_scales,
            "gate_logits": bf(gate / s[:, None]),
            "plan": bf(np.random.randn(B, N) * sigma)}


def reference(x_words, x_scales, e_words, e_scales, f_words, f_scales, gate_logits, plan):
    X = unpack_weight(x_words, x_scales, "e4m3")
    E = unpack4(e_words, e_scales)
    F = unpack_weight(f_words, f_scales, "e4m3")
    L = mxq(f64(gate_logits), 0)
    step = X.T @ E
    shift = X.T @ F
    logit = X.T @ L
    gated = step / (1.0 + np.exp(-logit))
    y = f64(plan) + gated + shift
    words, scales = planes(y.T)
    return y, words, scales

@@ -1,0 +1,346 @@
+from contextlib import ExitStack
+
+import concourse.mybir as mybir
+from concourse.masks import make_identity
+
+B, K, N = 768, 1536, 1024
+FLOPS = 3 * 2 * B * K * N
+
+F32 = mybir.dt.float32
+BF16 = mybir.dt.bfloat16
+U32 = mybir.dt.uint32
+I32 = mybir.dt.int32
+U8 = mybir.dt.uint8
+FP8X4 = mybir.dt.float8_e4m3fn_x4
+FP4X4 = mybir.dt.float4_e2m1fn_x4
+ADD = mybir.AluOpType.add
+MULT = mybir.AluOpType.mult
+SIGMOID = mybir.ActivationFunctionType.Sigmoid
+
+P = 128
+PASSES = K // 512
+HALF = 512
+ROW_TILES = B // P
+BANKS = 8
+F_SCALE_ROW = 4
+EARLY = 2
+HEAD = 4
+VEC_COLS = [[320, 320, 320], [512, 0, 0]]
+GROUPS = [(0, 0, 2), (0, 2, 2), (0, 4, 2), (1, 0, 2), (1, 2, 2), (1, 4, 1), (1, 5, 1)]
+HEAD_ORDER = [("logit", 0), ("logit", 1), ("step", 0), ("step", 1), ("logit", 2), ("step", 2)]
+TENSOR = "L04 L05 S04 S05 F00 F01 F02 F03 F04 F05 F10 F11 L10 L11 S10 T00 T02 L12 S11 L13 S12 L14 S13 T04 T10 L15 S14 F12 S15 F13 F14 F15 T12 T14 T15"
+VECTOR = "I00 Q00 I01 Q01 I02 Q02 I10 Q10 g00 g01 p00 g02 p01 g03 p02 g04 p03 g05 y00 p04 y01 I11 Q11 p05 y02 y03 I12 Q12 y04 y05 p10 p11 g10 g11 y10 q00 q02 y11 g12 g13 p12 p13 q04 g14 q10 y12 p14 g15 y13 p15 r14 r15 y14 y15 q12 q14 q15"
+SCALAR = "I00 I01 I02 I10 s00 s01 s02 s03 s04 s05 I11 I12 c00 c01 c02 c03 s10 s11 c04 R00 c05 R02 s12 c10 s13 c11 s14 R04 R10 s15 c12 c13 R12 R14 R15 Z12 Z13"
+GPSIMD = ""
+SYNC = "l00 x00 k00 l01 x01 e00 l02 x02 l10 X00 P00 j00 f00 P01 l11 l12 f10 P10 e10 P11 Y00 Y01 Y02 Y03 Y04 Y05 Y10 W00 W02 Y11 W04 Z00 Z01 Z02 Z03 W10 Y12 Y13 Y14 Y15 w12 Z10 Z11"
+
+
+def tile_mppi_gated_plan_update_k3_kernel(
+    tc, x_words, x_scales, e_words, e_scales, f_words, f_scales, gate_logits, plan, out_0, out_1, out_2
+):
+    nc = tc.nc
+    with ExitStack() as ctx:
+        keep = ctx.enter_context(tc.tile_pool(name="keep", bufs=1))
+        psum = ctx.enter_context(tc.psum_pool(name="psum", bufs=1))
+        ctx.enter_context(tc.manual_schedule())
+
+        def sbuf(name, shape, dtype, tag=None):
+            return keep.tile(shape, dtype, name=name, tag=tag or name, align_bytes=64)
+
+        halves = range(2)
+        passes = range(PASSES)
+        rows = range(ROW_TILES)
+        ident = sbuf("ident", [P, P], F32)
+        warm = sbuf("warm", [P, 1], F32)
+        x_codes = [sbuf("x_codes%d" % g, [P, HEAD * P], U32) for g in passes]
+        x_rest = sbuf("x_rest", [P, PASSES, B - HEAD * P], U32)
+        x_plane = sbuf("x_plane", [P, PASSES, B], U8)
+        e_plane = sbuf("e_plane", [P, PASSES, N], U8)
+        f_plane = sbuf("f_plane", [P, PASSES, N], U8)
+        e_codes = [sbuf("e_codes%d" % h, [P, PASSES, 2 * HALF], U8) for h in halves]
+        f_codes = [sbuf("f_codes%d" % h, [P, PASSES, HALF], U32) for h in halves]
+        plan_sb = [[sbuf("plan%d%d" % (h, s), [P, 3, HALF], BF16) for s in range(2)] for h in halves]
+        l_raw = [[sbuf("l_raw%d%d" % (h, g), [P, 4, HALF], BF16) for g in passes] for h in halves]
+        l_grouped = [[sbuf("l_grp%d%d" % (h, g), [P, HALF, 4], BF16) for g in passes] for h in halves]
+        l_codes = [[sbuf("l_codes%d%d" % (h, g), [P, HALF], U32) for g in passes] for h in halves]
+        l_plane = [[sbuf("l_plane%d%d" % (h, g), [P, HALF], U8) for g in passes] for h in halves]
+        y_codes = [sbuf("y_codes%d" % h, [P, B], U32) for h in halves]
+        y_plane = [sbuf("y_plane%d" % h, [P, B], U8) for h in halves]
+        live = {}
+
+        def cols(h):
+            return slice(h * HALF, (h + 1) * HALF)
+
+        def tile_rows(b):
+            return slice(b * P, (b + 1) * P)
+
+        def load_l(h, g):
+            src = gate_logits[g * 512 : (g + 1) * 512, cols(h)].rearrange("(p t) n -> p t n", t=4)
+            nc.sync.dma_start(out=l_raw[h][g][:], in_=src)
+
+        def load_x(g):
+            src = x_words[g].rearrange("p m t -> p (m t)").bitcast(I32)[:, : HEAD * P]
+            nc.sync.dma_start(out=x_codes[g][:].bitcast(I32), in_=src)
+
+        def load_x_rest():
+            src = x_words.rearrange("g p m t -> p g (m t)").bitcast(I32)[:, :, HEAD * P :]
+            nc.sync.dma_start(out=x_rest[:].bitcast(I32), in_=src)
+
+        def load_scales(engine, plane, scales, first_row):
+            for r in range(4):
+                src = scales.bitcast(I32)[:, r:16:4, :].rearrange("g q n -> q g n")
+                engine.dma_start(out=plane[first_row + r : P : 32, :, :].bitcast(I32), in_=src)
+
+        def load_e(h):
+            src = e_words.bitcast(I32)[:, :, h * 256 : (h + 1) * 256].rearrange("g p c -> p g c")
+            nc.sync.dma_start(out=e_codes[h][:].bitcast(I32), in_=src)
+
+        def load_f(h):
+            src = f_words.rearrange("g p n t -> p g (n t)").bitcast(I32)[:, :, cols(h)]
+            nc.sync.dma_start(out=f_codes[h][:].bitcast(I32), in_=src)
+
+        def load_plan(h, s):
+            src = plan[s * 3 * P : (s + 1) * 3 * P, cols(h)].rearrange("(b p) n -> p b n", p=P)
+            nc.sync.dma_start(out=plan_sb[h][s][:], in_=src)
+
+        def clear(plane):
+            nc.vector.memset(plane[:].rearrange("p g n -> p (g n)").bitcast(I32), 0)
+
+        def interleave(engine, h, g):
+            split = VEC_COLS[h][g]
+            ranges = [(c, min(c + 256, split)) for c in range(0, split, 256)] if engine == "vector" else [(split, HALF)][: HALF - split]
+            for c0, c1 in ranges:
+                dst = l_grouped[h][g][:, c0:c1, :].rearrange("p (c i) t -> p c t i", i=4)
+                src = l_raw[h][g][:, :, c0:c1].rearrange("p t (c i) -> p c t i", i=4)
+                if engine == "vector":
+                    nc.vector.tensor_copy(out=dst, in_=src)
+                else:
+                    nc.scalar.copy(out=dst, in_=src)
+
+        def quantise_l(h, g):
+            width = 256 if h == 0 else HALF
+            for c0 in range(0, HALF, width):
+                nc.vector.quantize_mx(
+                    out=l_codes[h][g][:, c0 : c0 + width].bitcast(FP8X4),
+                    scales=l_plane[h][g][:, c0 : c0 + width],
+                    in_=l_grouped[h][g][:, c0 : c0 + width, :].rearrange("p n t -> p (n t)"),
+                )
+
+        def product_pass(kind, h, b, g, bank):
+            if g == 0:
+                live[kind, h, b] = psum.tile([P, HALF], F32, name="%s%d%d" % (kind, h, b), tag="bank%d" % bank)
+            if kind == "logit":
+                rhs, rhs_scale = l_codes[h][g][:].bitcast(FP8X4), l_plane[h][g][:]
+            elif kind == "step":
+                rhs, rhs_scale = e_codes[h][:, g, :].bitcast(FP4X4), e_plane[:, g, cols(h)]
+            else:
+                rhs, rhs_scale = f_codes[h][:, g, :].bitcast(FP8X4), f_plane[F_SCALE_ROW:P, g, cols(h)]
+            x_tile = x_codes[g][:, tile_rows(b)] if b < HEAD else x_rest[:, g, tile_rows(b - HEAD)]
+            nc.tensor.matmul_mx(
+                out=live[kind, h, b][:],
+                lhsT=x_tile.bitcast(FP8X4),
+                lhsT_scale=x_plane[:, g, tile_rows(b)],
+                rhs=rhs,
+                rhs_scale=rhs_scale,
+                start=(g == 0),
+                stop=(g == PASSES - 1),
+            )
+
+        def plan_tile(h, b):
+            return plan_sb[h][b // 3][:, b % 3, :]
+
+        def sigmoid(h, b):
+            live["gate", h, b] = sbuf("gate%d%d" % (h, b), [P, HALF], F32, tag="gate%d" % b)
+            nc.scalar.activation(out=live["gate", h, b][:], in_=live["logit", h, b][:], func=SIGMOID)
+
+        def gate_step(h, b):
+            live["gated", h, b] = sbuf("gated%d%d" % (h, b), [P, HALF], F32, tag="gated%d" % b)
+            nc.vector.tensor_tensor(
+                out=live["gated", h, b][:], in0=live["step", h, b][:], in1=live["gate", h, b][:], op=MULT
+            )
+
+        def shift_is_early(h, b):
+            return h == 1 and b < EARLY
+
+        def add_plan(engine, h, b):
+            first = live["shift" if shift_is_early(h, b) else "gated", h, b]
+            live["part", h, b] = sbuf("part%d%d" % (h, b), [P, HALF], F32, tag="part%d" % b)
+            engine.tensor_tensor(out=live["part", h, b][:], in0=first[:], in1=plan_tile(h, b), op=ADD)
+
+        def finish(engine, h, b):
+            last = live["gated" if shift_is_early(h, b) else "shift", h, b]
+            live["y", h, b] = sbuf("y%d%d" % (h, b), [P, HALF], F32)
+            engine.tensor_tensor(out=live["y", h, b][:], in0=last[:], in1=live["part", h, b][:], op=ADD)
+
+        def store_y(h, b):
+            nc.sync.dma_start(out=out_0[tile_rows(b), cols(h)], in_=live["y", h, b][:])
+
+        def round_y(h, b):
+            live["y16", h, b] = sbuf("yr%d%d" % (h, b), [P, 2, P, 2], BF16, tag="yr%d" % b)
+            src = live["y", h, b][:].rearrange("m (p u e) -> m u p e", u=2, e=2)
+            nc.scalar.copy(out=live["y16", h, b][:], in_=src)
+
+        def finish_rounded(h, b):
+            live["y16", h, b] = sbuf("yr%d%d" % (h, b), [P, 2, P, 2], BF16, tag="yr%d" % b)
+            nc.vector.tensor_tensor(
+                out=live["y16", h, b][:],
+                in0=live["shift", h, b][:].rearrange("m (p u e) -> m u p e", u=2, e=2),
+                in1=live["part", h, b][:].rearrange("m (p u e) -> m u p e", u=2, e=2),
+                op=ADD,
+            )
+
+        def turn(h, b0, count, bank):
+            live["turned", h, b0] = psum.tile([P, count, 2, P], F32, name="turn%d%d" % (h, b0), tag="bank%d" % bank)
+            for s in range(count):
+                words = live["y16", h, b0 + s][:].rearrange("m u p e -> m (u p e)").bitcast(F32)
+                for u in range(2):
+                    nc.tensor.transpose(live["turned", h, b0][:, s, u, :], words[:, u * P : (u + 1) * P], ident[:])
+
+        def regroup(engine, h, b0, count):
+            live["yt", h, b0] = sbuf("yt%d%d" % (h, b0), [P, count * P * 4], BF16)
+            dst = live["yt", h, b0][:].bitcast(F32).rearrange("p (s m u) -> p s m u", s=count, u=2)
+            src = live["turned", h, b0][:].rearrange("p s u m -> p s m u")
+            if engine == "vector":
+                nc.vector.tensor_copy(out=dst, in_=src)
+            else:
+                nc.scalar.copy(out=dst, in_=src)
+
+        def quantise_y(h, b0, count):
+            m = slice(b0 * P, (b0 + count) * P)
+            nc.vector.quantize_mx(out=y_codes[h][:, m].bitcast(FP8X4), scales=y_plane[h][:, m], in_=live["yt", h, b0][:])
+
+        def store_codes(h, b0, count):
+            m = slice(b0 * P, (b0 + count) * P)
+            dst = out_1[h].rearrange("p m t -> p (m t)").bitcast(I32)[:, m]
+            nc.sync.dma_start(out=dst, in_=y_codes[h][:, m].bitcast(I32))
+
+        def store_scales(engine, h, quadrant):
+            dst = out_2[h].bitcast(I32)[4 * quadrant : 4 * quadrant + 4, :]
+            engine.dma_start(out=dst, in_=y_plane[h][32 * quadrant : 32 * quadrant + 4, :].bitcast(I32))
+
+        queues = {"vector": [], "gpsimd": [], "sync": [], "scalar": [], "tensor": []}
+
+        def put(queue, key, needs, call, *args):
+            queues[queue].append((key, needs, call, args))
+
+        bank_uses = []
+
+        def take_bank(emptied_by):
+            bank_uses.append(emptied_by)
+            count = len(bank_uses) - 1
+            return count % BANKS, ([bank_uses[count - BANKS]] if count >= BANKS else [])
+
+        def emptier(kind, h, b):
+            if kind == "logit":
+                return ("sigmoid", h, b)
+            if kind == "step":
+                return ("gated", h, b)
+            return ("part", h, b) if shift_is_early(h, b) else ("y", h, b)
+
+        def operand_needs(kind, h, g):
+            if kind == "logit":
+                return [("ql", h, g)]
+            if kind == "step":
+                return [("e", h), "e_scales"]
+            return [("f", h), "f_scales"]
+
+        def put_pass(kind, h, b, g, bank, waits):
+            x_need = ("x", g) if b < HEAD else "x_rest"
+            put("tensor", (kind, h, b, g), [x_need, "x_scales"] + operand_needs(kind, h, g) + waits,
+                product_pass, kind, h, b, g, bank)
+
+        def put_product(kind, h, b):
+            bank, waits = take_bank(emptier(kind, h, b))
+            for g in passes:
+                put_pass(kind, h, b, g, bank, waits)
+
+        def group_of(h, b):
+            return [(h, b0) for (hh, b0, count) in GROUPS if hh == h and b0 <= b < b0 + count][0]
+
+        def put_token(queue, token):
+            op, h, b = token[0], int(token[1]), int(token[2])
+            engine = {"vector": nc.vector, "gpsimd": nc.gpsimd, "scalar": nc.scalar, "sync": nc.sync, "tensor": nc.tensor}[queue]
+            count = ([c for (hh, b0, c) in GROUPS if (hh, b0) == (h, b)] + [0])[0]
+            if op in "LSF":
+                put_product({"L": "logit", "S": "step", "F": "shift"}[op], h, b)
+            elif op == "T":
+                bank, waits = take_bank(("yt", h, b))
+                put(queue, ("turned", h, b), [("y16", h, b + s) for s in range(count)] + ["ident"] + waits,
+                    turn, h, b, count, bank)
+            elif op == "g":
+                put(queue, ("gated", h, b), [("step", h, b, 2), ("sigmoid", h, b)] + ([("part", 0, b)] if h else []),
+                    gate_step, h, b)
+            elif op == "p":
+                first = ("shift", h, b, 2) if shift_is_early(h, b) else ("gated", h, b)
+                put(queue, ("part", h, b), [first, ("plan", h, b // 3)] + ([("y", 0, b)] if h else []), add_plan, engine, h, b)
+            elif op == "y":
+                last = ("gated", h, b) if shift_is_early(h, b) else ("shift", h, b, 2)
+                put(queue, ("y", h, b), [last, ("part", h, b)], finish, engine, h, b)
+            elif op == "r":
+                put(queue, ("y16", h, b), [("shift", h, b, 2), ("part", h, b), ("turned",) + group_of(0, b)], finish_rounded, h, b)
+            elif op == "Q":
+                put(queue, ("ql", h, b), [("il", h, b, "scalar"), ("il", h, b, "vector")], quantise_l, h, b)
+            elif op == "I":
+                put(queue, ("il", h, b, queue), [("l", h, b)], interleave, queue, h, b)
+            elif op == "q":
+                put(queue, ("qy", h, b), [("yt", h, b)], quantise_y, h, b, count)
+            elif op == "s":
+                put(queue, ("sigmoid", h, b), [("logit", h, b, 2)] + ([("gated", 0, b)] if h else []), sigmoid, h, b)
+            elif op == "c":
+                put(queue, ("y16", h, b), [("y", h, b)] + ([("turned",) + group_of(0, b)] if h else []), round_y, h, b)
+            elif op == "R":
+                put(queue, ("yt", h, b), [("turned", h, b)], regroup, queue, h, b, count)
+            elif op == "Y":
+                put(queue, ("store_y", h, b), [("y", h, b)], store_y, h, b)
+            elif op == "W":
+                put(queue, ("codes", h, b), [("qy", h, b)], store_codes, h, b, count)
+            elif op == "w":
+                put(queue, ("codes", h, b), [("qy", h, b0) for (hh, b0, c) in GROUPS if hh == h and b0 >= b],
+                    store_codes, h, b, ROW_TILES - b)
+            elif op == "Z":
+                put(queue, ("scales", h, b), [("qy", hh, b0) for (hh, b0, c) in GROUPS if hh == h], store_scales, engine, h, b)
+            elif op == "l":
+                put(queue, ("l", h, b), [], load_l, h, b)
+            elif op == "x":
+                put(queue, ("x", b), [], load_x, b)
+            elif op == "X":
+                put(queue, "x_rest", [], load_x_rest)
+            elif op == "e":
+                put(queue, ("e", h), [], load_e, h)
+            elif op == "f":
+                put(queue, ("f", h), [], load_f, h)
+            elif op == "P":
+                put(queue, ("plan", h, b), [], load_plan, h, b)
+            elif op == "j":
+                put(queue, "f_scales", ["clear_f"], load_scales, nc.sync, f_plane, f_scales, F_SCALE_ROW)
+            else:
+                put(queue, "x_scales", ["clear_x"], load_scales, nc.sync, x_plane, x_scales, 0)
+
+        put("vector", "clear_e", [], clear, e_plane)
+        put("vector", "clear_x", [], clear, x_plane)
+        put("vector", "clear_f", [], clear, f_plane)
+        put("gpsimd", "ident", [], make_identity, nc, ident[:])
+        put("gpsimd", "e_scales", ["clear_e"], load_scales, nc.gpsimd, e_plane, e_scales, 0)
+        put("scalar", "warm", ["ident"], nc.scalar.activation, warm[:], ident[:, 0:1], SIGMOID)
+
+        head_banks = {(kind, b): take_bank(emptier(kind, 0, b))[0] for kind in ("logit", "step") for b in range(HEAD)}
+        for kind, g in HEAD_ORDER:
+            for b in range(HEAD):
+                put_pass(kind, 0, b, g, head_banks[kind, b], [])
+
+        for queue, order in (("tensor", TENSOR), ("vector", VECTOR), ("scalar", SCALAR), ("gpsimd", GPSIMD), ("sync", SYNC)):
+            for token in order.split():
+                put_token(queue, token)
+
+        written = set()
+        heads = {name: 0 for name in queues}
+        total = sum(len(q) for q in queues.values())
+        while len(written) < total:
+            before = len(written)
+            for name, queue in queues.items():
+                while heads[name] < len(queue) and all(need in written for need in queue[heads[name]][1]):
+                    key, needs, call, args = queue[heads[name]]
+                    call(*args)
+                    written.add(key)
+                    heads[name] += 1
+            assert len(written) > before, [queues[n][heads[n]][:2] for n in queues if heads[n] < len(queues[n])]

@@ -23,16 +23,15 @@ HALF = 512
 ROW_TILES = B // P
 BANKS = 8
 F_SCALE_ROW = 4
-EARLY = 2
 HEAD = 4
 VEC_COLS = [[320, 320, 320], [512, 0, 0]]
 GROUPS = [(0, 0, 2), (0, 2, 2), (0, 4, 2), (1, 0, 2), (1, 2, 2), (1, 4, 1), (1, 5, 1)]
-HEAD_ORDER = [("logit", 0), ("logit", 1), ("step", 0), ("step", 1), ("logit", 2), ("step", 2)]
-TENSOR = "L04 L05 S04 S05 F00 F01 F02 F03 F04 F05 F10 F11 L10 L11 S10 T00 T02 L12 S11 L13 S12 L14 S13 T04 T10 L15 S14 F12 S15 F13 F14 F15 T12 T14 T15"
-VECTOR = "I00 Q00 I01 Q01 I02 Q02 I10 Q10 g00 g01 p00 g02 p01 g03 p02 g04 p03 g05 y00 p04 y01 I11 Q11 p05 y02 y03 I12 Q12 y04 y05 p10 p11 g10 g11 y10 q00 q02 y11 g12 g13 p12 p13 q04 g14 q10 y12 p14 g15 y13 p15 r14 r15 y14 y15 q12 q14 q15"
-SCALAR = "I00 I01 I02 I10 s00 s01 s02 s03 s04 s05 I11 I12 c00 c01 c02 c03 s10 s11 c04 R00 c05 R02 s12 c10 s13 c11 s14 R04 R10 s15 c12 c13 R12 R14 R15 Z12 Z13"
+HEAD_ORDER = [("logit", 0), ("step", 0), ("step", 1), ("logit", 1), ("step", 2), ("logit", 2)]
+TENSOR = "L04 L05 S04 S05 F00 F01 F02 F03 F04 F05 S10 S11 L10 L11 L12 L13 S12 S13 L14 S14 T00 T02 F10 F11 F12 L15 T04 F13 S15 F14 T10 F15 T12 T14 T15"
+VECTOR = "I00 Q00 I01 Q01 I02 Q02 I10 Q10 g00 g01 g02 g03 g04 g05 p00 p01 I11 Q11 y00 p02 y01 p03 I12 Q12 p04 y02 p05 y03 g10 g11 y04 y05 p10 g12 p11 g13 p12 g14 y10 p13 q00 y11 q02 y12 p14 y13 q04 g15 y14 p15 q10 r15 y15 q12 q14 q15"
+SCALAR = "I00 I01 I02 I10 s00 s01 s02 s03 s04 s05 I11 I12 c00 c01 s10 s11 c02 s12 c03 s13 s14 c04 c05 R00 R02 c10 s15 c11 R04 c12 c13 R10 c14 R12 R14 R15 Z12 Z13"
 GPSIMD = ""
-SYNC = "l00 x00 k00 l01 x01 e00 l02 x02 l10 X00 P00 j00 f00 P01 l11 l12 f10 P10 e10 P11 Y00 Y01 Y02 Y03 Y04 Y05 Y10 W00 W02 Y11 W04 Z00 Z01 Z02 Z03 W10 Y12 Y13 Y14 Y15 w12 Z10 Z11"
+SYNC = "l00 x00 k00 i00 e00 l01 x01 e01 l02 x02 e02 l10 X00 j00 f00 l11 P00 l12 i10 e10 P01 P10 j10 f10 P11 Y00 Y01 Y02 Y03 Y04 Y05 Y10 W00 W02 Y11 Y12 Y13 W04 Z00 Z01 Z02 Z03 Y14 W10 Y15 v12 W15 Z10 Z11"
 
 
 def tile_mppi_gated_plan_update_k3_kernel(
@@ -51,13 +50,15 @@ def tile_mppi_gated_plan_update_k3_kernel(
         passes = range(PASSES)
         rows = range(ROW_TILES)
         ident = sbuf("ident", [P, P], F32)
+        warm_in = sbuf("warm_in", [P, 1], F32)
         warm = sbuf("warm", [P, 1], F32)
         x_codes = [sbuf("x_codes%d" % g, [P, HEAD * P], U32) for g in passes]
         x_rest = sbuf("x_rest", [P, PASSES, B - HEAD * P], U32)
         x_plane = sbuf("x_plane", [P, PASSES, B], U8)
-        e_plane = sbuf("e_plane", [P, PASSES, N], U8)
-        f_plane = sbuf("f_plane", [P, PASSES, N], U8)
-        e_codes = [sbuf("e_codes%d" % h, [P, PASSES, 2 * HALF], U8) for h in halves]
+        e_plane = [sbuf("e_plane%d" % h, [P, PASSES, HALF], U8) for h in halves]
+        f_plane = [sbuf("f_plane%d" % h, [P, PASSES, HALF], U8) for h in halves]
+        e_first = [sbuf("e_first%d" % g, [P, 2 * HALF], U8) for g in passes]
+        e_second = sbuf("e_second", [P, PASSES, 2 * HALF], U8)
         f_codes = [sbuf("f_codes%d" % h, [P, PASSES, HALF], U32) for h in halves]
         plan_sb = [[sbuf("plan%d%d" % (h, s), [P, 3, HALF], BF16) for s in range(2)] for h in halves]
         l_raw = [[sbuf("l_raw%d%d" % (h, g), [P, 4, HALF], BF16) for g in passes] for h in halves]
@@ -86,14 +87,17 @@ def tile_mppi_gated_plan_update_k3_kernel(
             src = x_words.rearrange("g p m t -> p g (m t)").bitcast(I32)[:, :, HEAD * P :]
             nc.sync.dma_start(out=x_rest[:].bitcast(I32), in_=src)
 
-        def load_scales(engine, plane, scales, first_row):
+        def load_scales(plane, scales, first_row):
             for r in range(4):
                 src = scales.bitcast(I32)[:, r:16:4, :].rearrange("g q n -> q g n")
-                engine.dma_start(out=plane[first_row + r : P : 32, :, :].bitcast(I32), in_=src)
+                nc.sync.dma_start(out=plane[first_row + r : P : 32, :, :].bitcast(I32), in_=src)
 
-        def load_e(h):
-            src = e_words.bitcast(I32)[:, :, h * 256 : (h + 1) * 256].rearrange("g p c -> p g c")
-            nc.sync.dma_start(out=e_codes[h][:].bitcast(I32), in_=src)
+        def load_e(h, g):
+            if h == 0:
+                nc.sync.dma_start(out=e_first[g][:].bitcast(I32), in_=e_words[g].bitcast(I32)[:, :256])
+            else:
+                src = e_words.bitcast(I32)[:, :, 256:].rearrange("g p c -> p g c")
+                nc.sync.dma_start(out=e_second[:].bitcast(I32), in_=src)
 
         def load_f(h):
             src = f_words.rearrange("g p n t -> p g (n t)").bitcast(I32)[:, :, cols(h)]
@@ -132,9 +136,10 @@ def tile_mppi_gated_plan_update_k3_kernel(
             if kind == "logit":
                 rhs, rhs_scale = l_codes[h][g][:].bitcast(FP8X4), l_plane[h][g][:]
             elif kind == "step":
-                rhs, rhs_scale = e_codes[h][:, g, :].bitcast(FP4X4), e_plane[:, g, cols(h)]
+                e_tile = e_first[g][:] if h == 0 else e_second[:, g, :]
+                rhs, rhs_scale = e_tile.bitcast(FP4X4), e_plane[h][:, g, :]
             else:
-                rhs, rhs_scale = f_codes[h][:, g, :].bitcast(FP8X4), f_plane[F_SCALE_ROW:P, g, cols(h)]
+                rhs, rhs_scale = f_codes[h][:, g, :].bitcast(FP8X4), f_plane[h][F_SCALE_ROW:P, g, :]
             x_tile = x_codes[g][:, tile_rows(b)] if b < HEAD else x_rest[:, g, tile_rows(b - HEAD)]
             nc.tensor.matmul_mx(
                 out=live[kind, h, b][:],
@@ -159,18 +164,15 @@ def tile_mppi_gated_plan_update_k3_kernel(
                 out=live["gated", h, b][:], in0=live["step", h, b][:], in1=live["gate", h, b][:], op=MULT
             )
 
-        def shift_is_early(h, b):
-            return h == 1 and b < EARLY
-
-        def add_plan(engine, h, b):
-            first = live["shift" if shift_is_early(h, b) else "gated", h, b]
+        def first_sum(engine, h, b):
+            pair = (live["shift", h, b][:], live["gated", h, b][:]) if h == 0 else (live["gated", h, b][:], plan_tile(h, b))
             live["part", h, b] = sbuf("part%d%d" % (h, b), [P, HALF], F32, tag="part%d" % b)
-            engine.tensor_tensor(out=live["part", h, b][:], in0=first[:], in1=plan_tile(h, b), op=ADD)
+            engine.tensor_tensor(out=live["part", h, b][:], in0=pair[0], in1=pair[1], op=ADD)
 
         def finish(engine, h, b):
-            last = live["gated" if shift_is_early(h, b) else "shift", h, b]
+            pair = (live["part", h, b][:], plan_tile(h, b)) if h == 0 else (live["shift", h, b][:], live["part", h, b][:])
             live["y", h, b] = sbuf("y%d%d" % (h, b), [P, HALF], F32)
-            engine.tensor_tensor(out=live["y", h, b][:], in0=last[:], in1=live["part", h, b][:], op=ADD)
+            engine.tensor_tensor(out=live["y", h, b][:], in0=pair[0], in1=pair[1], op=ADD)
 
         def store_y(h, b):
             nc.sync.dma_start(out=out_0[tile_rows(b), cols(h)], in_=live["y", h, b][:])
@@ -235,14 +237,14 @@ def tile_mppi_gated_plan_update_k3_kernel(
                 return ("sigmoid", h, b)
             if kind == "step":
                 return ("gated", h, b)
-            return ("part", h, b) if shift_is_early(h, b) else ("y", h, b)
+            return ("part", h, b) if h == 0 else ("y", h, b)
 
         def operand_needs(kind, h, g):
             if kind == "logit":
                 return [("ql", h, g)]
             if kind == "step":
-                return [("e", h), "e_scales"]
-            return [("f", h), "f_scales"]
+                return [("e", h, g if h == 0 else 0), ("e_scales", h)]
+            return [("f", h), ("f_scales", h)]
 
         def put_pass(kind, h, b, g, bank, waits):
             x_need = ("x", g) if b < HEAD else "x_rest"
@@ -271,10 +273,10 @@ def tile_mppi_gated_plan_update_k3_kernel(
                 put(queue, ("gated", h, b), [("step", h, b, 2), ("sigmoid", h, b)] + ([("part", 0, b)] if h else []),
                     gate_step, h, b)
             elif op == "p":
-                first = ("shift", h, b, 2) if shift_is_early(h, b) else ("gated", h, b)
-                put(queue, ("part", h, b), [first, ("plan", h, b // 3)] + ([("y", 0, b)] if h else []), add_plan, engine, h, b)
+                other = [("shift", h, b, 2)] if h == 0 else [("plan", h, b // 3), ("y", 0, b)]
+                put(queue, ("part", h, b), [("gated", h, b)] + other, first_sum, engine, h, b)
             elif op == "y":
-                last = ("gated", h, b) if shift_is_early(h, b) else ("shift", h, b, 2)
+                last = ("plan", h, b // 3) if h == 0 else ("shift", h, b, 2)
                 put(queue, ("y", h, b), [last, ("part", h, b)], finish, engine, h, b)
             elif op == "r":
                 put(queue, ("y16", h, b), [("shift", h, b, 2), ("part", h, b), ("turned",) + group_of(0, b)], finish_rounded, h, b)
@@ -306,22 +308,28 @@ def tile_mppi_gated_plan_update_k3_kernel(
             elif op == "X":
                 put(queue, "x_rest", [], load_x_rest)
             elif op == "e":
-                put(queue, ("e", h), [], load_e, h)
+                put(queue, ("e", h, b), [], load_e, h, b)
             elif op == "f":
                 put(queue, ("f", h), [], load_f, h)
             elif op == "P":
                 put(queue, ("plan", h, b), [], load_plan, h, b)
             elif op == "j":
-                put(queue, "f_scales", ["clear_f"], load_scales, nc.sync, f_plane, f_scales, F_SCALE_ROW)
+                put(queue, ("f_scales", h), [("clear_f", h)], load_scales, f_plane[h], f_scales[:, :, cols(h)], F_SCALE_ROW)
+            elif op == "i":
+                put(queue, ("e_scales", h), [("clear_e", h)], load_scales, e_plane[h], e_scales[:, :, cols(h)], 0)
+            elif op == "v":
+                put(queue, ("codes", h, b), [("qy", h, b0) for (hh, b0, c) in GROUPS if hh == h and b <= b0 < 5],
+                    store_codes, h, b, 5 - b)
             else:
-                put(queue, "x_scales", ["clear_x"], load_scales, nc.sync, x_plane, x_scales, 0)
+                put(queue, "x_scales", ["clear_x"], load_scales, x_plane, x_scales, 0)
 
-        put("vector", "clear_e", [], clear, e_plane)
+        put("vector", "warm_in", [], nc.vector.memset, warm_in[:], 0.0)
         put("vector", "clear_x", [], clear, x_plane)
-        put("vector", "clear_f", [], clear, f_plane)
+        for h in halves:
+            put("vector", ("clear_e", h), [], clear, e_plane[h])
+            put("vector", ("clear_f", h), [], clear, f_plane[h])
         put("gpsimd", "ident", [], make_identity, nc, ident[:])
-        put("gpsimd", "e_scales", ["clear_e"], load_scales, nc.gpsimd, e_plane, e_scales, 0)
-        put("scalar", "warm", ["ident"], nc.scalar.activation, warm[:], ident[:, 0:1], SIGMOID)
+        put("scalar", "warm", ["warm_in"], nc.scalar.activation, warm[:], warm_in[:], SIGMOID)
 
         head_banks = {(kind, b): take_bank(emptier(kind, 0, b))[0] for kind in ("logit", "step") for b in range(HEAD)}
         for kind, g in HEAD_ORDER:

@@ -24,14 +24,15 @@ ROW_TILES = B // P
 BANKS = 8
 F_SCALE_ROW = 4
 HEAD = 4
+WARM_PASSES = 26
 VEC_COLS = [[320, 320, 320], [512, 0, 0]]
 GROUPS = [(0, 0, 2), (0, 2, 2), (0, 4, 2), (1, 0, 2), (1, 2, 2), (1, 4, 1), (1, 5, 1)]
-HEAD_ORDER = [("logit", 0), ("step", 0), ("step", 1), ("logit", 1), ("step", 2), ("logit", 2)]
-TENSOR = "L04 L05 S04 S05 F00 F01 F02 F03 F04 F05 S10 S11 L10 L11 L12 L13 S12 S13 L14 S14 T00 T02 F10 F11 F12 L15 T04 F13 S15 F14 T10 F15 T12 T14 T15"
-VECTOR = "I00 Q00 I01 Q01 I02 Q02 I10 Q10 g00 g01 g02 g03 g04 g05 p00 p01 I11 Q11 y00 p02 y01 p03 I12 Q12 p04 y02 p05 y03 g10 g11 y04 y05 p10 g12 p11 g13 p12 g14 y10 p13 q00 y11 q02 y12 p14 y13 q04 g15 y14 p15 q10 r15 y15 q12 q14 q15"
-SCALAR = "I00 I01 I02 I10 s00 s01 s02 s03 s04 s05 I11 I12 c00 c01 s10 s11 c02 s12 c03 s13 s14 c04 c05 R00 R02 c10 s15 c11 R04 c12 c13 R10 c14 R12 R14 R15 Z12 Z13"
-GPSIMD = ""
-SYNC = "l00 x00 k00 i00 e00 l01 x01 e01 l02 x02 e02 l10 X00 j00 f00 l11 P00 l12 i10 e10 P01 P10 j10 f10 P11 Y00 Y01 Y02 Y03 Y04 Y05 Y10 W00 W02 Y11 Y12 Y13 W04 Z00 Z01 Z02 Z03 Y14 W10 Y15 v12 W15 Z10 Z11"
+HEAD_ORDER = [("logit", 0), ("step", 0), ("logit", 1), ("step", 1), ("step", 2), ("logit", 2)]
+TENSOR = "L04 L05 S04 S05 F00 F01 F02 F03 F04 F05 S10 S11 L10 L11 L12 L13 S12 S13 F10 F11 T00 T02 T04 L14 S14 F12 L15 F13 S15 F14 T10 F15 T12 T14 T15"
+VECTOR = "I00 Q00 I01 Q01 I02 Q02 I10 g00 Q10 g01 g02 g03 g04 g05 p00 p01 p02 I11 Q11 p03 I12 Q12 y03 p04 y04 p05 g10 g11 y05 p10 p11 g12 y10 g13 y11 g14 q00 q02 q04 y12 y13 g15 y14 p15 q10 r15 y15 q12 q14 q15"
+SCALAR = "I00 I01 I02 I10 s00 s01 s02 s03 s04 s05 I11 I12 c00 c01 s10 s11 c02 s12 s13 c03 c04 c05 R00 s14 R02 R04 c10 c11 s15 c12 c13 R10 c14 R12 R14 R15 Z12 Z13"
+GPSIMD = "y00 y01 y02 p12 p13 p14"
+SYNC = "l00 x00 k00 l01 e00 i00 x01 e01 l02 x02 e02 l10 X00 j00 f00 l11 P00 l12 i10 e10 P01 P10 j10 f10 P11 Y00 Y01 Y02 Y03 Y04 Y05 Y10 Y11 W00 W02 Y12 Y13 W04 Z00 Z01 Z02 Z03 Y14 W10 Y15 v12 W15 Z10 Z11"
 
 
 def tile_mppi_gated_plan_update_k3_kernel(
@@ -52,6 +53,9 @@ def tile_mppi_gated_plan_update_k3_kernel(
         ident = sbuf("ident", [P, P], F32)
         warm_in = sbuf("warm_in", [P, 1], F32)
         warm = sbuf("warm", [P, 1], F32)
+        ones = sbuf("ones", [P, 4 * P], BF16)
+        ones_codes = sbuf("ones_codes", [P, P], U32)
+        ones_plane = sbuf("ones_plane", [P, P], U8)
         x_codes = [sbuf("x_codes%d" % g, [P, HEAD * P], U32) for g in passes]
         x_rest = sbuf("x_rest", [P, PASSES, B - HEAD * P], U32)
         x_plane = sbuf("x_plane", [P, PASSES, B], U8)
@@ -128,6 +132,19 @@ def tile_mppi_gated_plan_update_k3_kernel(
                     out=l_codes[h][g][:, c0 : c0 + width].bitcast(FP8X4),
                     scales=l_plane[h][g][:, c0 : c0 + width],
                     in_=l_grouped[h][g][:, c0 : c0 + width, :].rearrange("p n t -> p (n t)"),
+                )
+
+        def warm_tensor():
+            idle = psum.tile([P, P], F32, name="idle", tag="bank%d" % (BANKS - 1))
+            for i in range(WARM_PASSES):
+                nc.tensor.matmul_mx(
+                    out=idle[:],
+                    lhsT=ones_codes[:].bitcast(FP8X4),
+                    lhsT_scale=ones_plane[:],
+                    rhs=ones_codes[:].bitcast(FP8X4),
+                    rhs_scale=ones_plane[:],
+                    start=True,
+                    stop=True,
                 )
 
         def product_pass(kind, h, b, g, bank):
@@ -325,9 +342,13 @@ def tile_mppi_gated_plan_update_k3_kernel(
 
         put("vector", "warm_in", [], nc.vector.memset, warm_in[:], 0.0)
         put("vector", "clear_x", [], clear, x_plane)
-        for h in halves:
-            put("vector", ("clear_e", h), [], clear, e_plane[h])
-            put("vector", ("clear_f", h), [], clear, f_plane[h])
+        put("vector", "ones", [], nc.vector.memset, ones[:], 1.0)
+        put("vector", ("clear_e", 0), [], clear, e_plane[0])
+        put("vector", "ones_codes", [], nc.vector.quantize_mx, ones_codes[:].bitcast(FP8X4), ones_plane[:], ones[:])
+        put("vector", ("clear_f", 0), [], clear, f_plane[0])
+        put("vector", ("clear_e", 1), [], clear, e_plane[1])
+        put("vector", ("clear_f", 1), [], clear, f_plane[1])
+        put("tensor", "warm_tensor", ["ones_codes"], warm_tensor)
         put("gpsimd", "ident", [], make_identity, nc, ident[:])
         put("scalar", "warm", ["warm_in"], nc.scalar.activation, warm[:], warm_in[:], SIGMOID)
 

from contextlib import ExitStack

import concourse.mybir as mybir
from concourse.masks import make_identity

B, K, N = 768, 1536, 1024
FLOPS = 3 * 2 * B * K * N

F32 = mybir.dt.float32
BF16 = mybir.dt.bfloat16
U32 = mybir.dt.uint32
I32 = mybir.dt.int32
U8 = mybir.dt.uint8
FP8X4 = mybir.dt.float8_e4m3fn_x4
FP4X4 = mybir.dt.float4_e2m1fn_x4
ADD = mybir.AluOpType.add
MULT = mybir.AluOpType.mult
SIGMOID = mybir.ActivationFunctionType.Sigmoid

P = 128
PASSES = K // 512
HALF = 512
ROW_TILES = B // P
BANKS = 8
F_SCALE_ROW = 4
HEAD = 4
WARM_PASSES = 26
VEC_COLS = [[320, 320, 320], [512, 0, 0]]
GROUPS = [(0, 0, 2), (0, 2, 2), (0, 4, 2), (1, 0, 2), (1, 2, 2), (1, 4, 1), (1, 5, 1)]
HEAD_ORDER = [("logit", 0), ("step", 0), ("logit", 1), ("step", 1), ("step", 2), ("logit", 2)]
TENSOR = "L04 L05 S04 S05 F00 F01 F02 F03 F04 F05 S10 S11 L10 L11 L12 L13 S12 S13 F10 F11 T00 T02 T04 L14 S14 F12 L15 F13 S15 F14 T10 F15 T12 T14 T15"
VECTOR = "I00 Q00 I01 Q01 I02 Q02 I10 g00 Q10 g01 g02 g03 g04 g05 p00 p01 p02 I11 Q11 p03 I12 Q12 y03 p04 y04 p05 g10 g11 y05 p10 p11 g12 y10 g13 y11 g14 q00 q02 q04 y12 y13 g15 y14 p15 q10 r15 y15 q12 q14 q15"
SCALAR = "I00 I01 I02 I10 s00 s01 s02 s03 s04 s05 I11 I12 c00 c01 s10 s11 c02 s12 s13 c03 c04 c05 R00 s14 R02 R04 c10 c11 s15 c12 c13 R10 c14 R12 R14 R15 Z12 Z13"
GPSIMD = "y00 y01 y02 p12 p13 p14"
SYNC = "l00 x00 k00 l01 e00 i00 x01 e01 l02 x02 e02 l10 X00 j00 f00 l11 P00 l12 i10 e10 P01 P10 j10 f10 P11 Y00 Y01 Y02 Y03 Y04 Y05 Y10 Y11 W00 W02 Y12 Y13 W04 Z00 Z01 Z02 Z03 Y14 W10 Y15 v12 W15 Z10 Z11"


def tile_mppi_gated_plan_update_k3_kernel(
    tc, x_words, x_scales, e_words, e_scales, f_words, f_scales, gate_logits, plan, out_0, out_1, out_2
):
    nc = tc.nc
    with ExitStack() as ctx:
        keep = ctx.enter_context(tc.tile_pool(name="keep", bufs=1))
        psum = ctx.enter_context(tc.psum_pool(name="psum", bufs=1))
        ctx.enter_context(tc.manual_schedule())

        def sbuf(name, shape, dtype, tag=None):
            return keep.tile(shape, dtype, name=name, tag=tag or name, align_bytes=64)

        halves = range(2)
        passes = range(PASSES)
        rows = range(ROW_TILES)
        ident = sbuf("ident", [P, P], F32)
        warm_in = sbuf("warm_in", [P, 1], F32)
        warm = sbuf("warm", [P, 1], F32)
        ones = sbuf("ones", [P, 4 * P], BF16)
        ones_codes = sbuf("ones_codes", [P, P], U32)
        ones_plane = sbuf("ones_plane", [P, P], U8)
        x_codes = [sbuf("x_codes%d" % g, [P, HEAD * P], U32) for g in passes]
        x_rest = sbuf("x_rest", [P, PASSES, B - HEAD * P], U32)
        x_plane = sbuf("x_plane", [P, PASSES, B], U8)
        e_plane = [sbuf("e_plane%d" % h, [P, PASSES, HALF], U8) for h in halves]
        f_plane = [sbuf("f_plane%d" % h, [P, PASSES, HALF], U8) for h in halves]
        e_first = [sbuf("e_first%d" % g, [P, 2 * HALF], U8) for g in passes]
        e_second = sbuf("e_second", [P, PASSES, 2 * HALF], U8)
        f_codes = [sbuf("f_codes%d" % h, [P, PASSES, HALF], U32) for h in halves]
        plan_sb = [[sbuf("plan%d%d" % (h, s), [P, 3, HALF], BF16) for s in range(2)] for h in halves]
        l_raw = [[sbuf("l_raw%d%d" % (h, g), [P, 4, HALF], BF16) for g in passes] for h in halves]
        l_grouped = [[sbuf("l_grp%d%d" % (h, g), [P, HALF, 4], BF16) for g in passes] for h in halves]
        l_codes = [[sbuf("l_codes%d%d" % (h, g), [P, HALF], U32) for g in passes] for h in halves]
        l_plane = [[sbuf("l_plane%d%d" % (h, g), [P, HALF], U8) for g in passes] for h in halves]
        y_codes = [sbuf("y_codes%d" % h, [P, B], U32) for h in halves]
        y_plane = [sbuf("y_plane%d" % h, [P, B], U8) for h in halves]
        live = {}

        def cols(h):
            return slice(h * HALF, (h + 1) * HALF)

        def tile_rows(b):
            return slice(b * P, (b + 1) * P)

        def load_l(h, g):
            src = gate_logits[g * 512 : (g + 1) * 512, cols(h)].rearrange("(p t) n -> p t n", t=4)
            nc.sync.dma_start(out=l_raw[h][g][:], in_=src)

        def load_x(g):
            src = x_words[g].rearrange("p m t -> p (m t)").bitcast(I32)[:, : HEAD * P]
            nc.sync.dma_start(out=x_codes[g][:].bitcast(I32), in_=src)

        def load_x_rest():
            src = x_words.rearrange("g p m t -> p g (m t)").bitcast(I32)[:, :, HEAD * P :]
            nc.sync.dma_start(out=x_rest[:].bitcast(I32), in_=src)

        def load_scales(plane, scales, first_row):
            for r in range(4):
                src = scales.bitcast(I32)[:, r:16:4, :].rearrange("g q n -> q g n")
                nc.sync.dma_start(out=plane[first_row + r : P : 32, :, :].bitcast(I32), in_=src)

        def load_e(h, g):
            if h == 0:
                nc.sync.dma_start(out=e_first[g][:].bitcast(I32), in_=e_words[g].bitcast(I32)[:, :256])
            else:
                src = e_words.bitcast(I32)[:, :, 256:].rearrange("g p c -> p g c")
                nc.sync.dma_start(out=e_second[:].bitcast(I32), in_=src)

        def load_f(h):
            src = f_words.rearrange("g p n t -> p g (n t)").bitcast(I32)[:, :, cols(h)]
            nc.sync.dma_start(out=f_codes[h][:].bitcast(I32), in_=src)

        def load_plan(h, s):
            src = plan[s * 3 * P : (s + 1) * 3 * P, cols(h)].rearrange("(b p) n -> p b n", p=P)
            nc.sync.dma_start(out=plan_sb[h][s][:], in_=src)

        def clear(plane):
            nc.vector.memset(plane[:].rearrange("p g n -> p (g n)").bitcast(I32), 0)

        def interleave(engine, h, g):
            split = VEC_COLS[h][g]
            ranges = [(c, min(c + 256, split)) for c in range(0, split, 256)] if engine == "vector" else [(split, HALF)][: HALF - split]
            for c0, c1 in ranges:
                dst = l_grouped[h][g][:, c0:c1, :].rearrange("p (c i) t -> p c t i", i=4)
                src = l_raw[h][g][:, :, c0:c1].rearrange("p t (c i) -> p c t i", i=4)
                if engine == "vector":
                    nc.vector.tensor_copy(out=dst, in_=src)
                else:
                    nc.scalar.copy(out=dst, in_=src)

        def quantise_l(h, g):
            width = 256 if h == 0 else HALF
            for c0 in range(0, HALF, width):
                nc.vector.quantize_mx(
                    out=l_codes[h][g][:, c0 : c0 + width].bitcast(FP8X4),
                    scales=l_plane[h][g][:, c0 : c0 + width],
                    in_=l_grouped[h][g][:, c0 : c0 + width, :].rearrange("p n t -> p (n t)"),
                )

        def warm_tensor():
            idle = psum.tile([P, P], F32, name="idle", tag="bank%d" % (BANKS - 1))
            for i in range(WARM_PASSES):
                nc.tensor.matmul_mx(
                    out=idle[:],
                    lhsT=ones_codes[:].bitcast(FP8X4),
                    lhsT_scale=ones_plane[:],
                    rhs=ones_codes[:].bitcast(FP8X4),
                    rhs_scale=ones_plane[:],
                    start=True,
                    stop=True,
                )

        def product_pass(kind, h, b, g, bank):
            if g == 0:
                live[kind, h, b] = psum.tile([P, HALF], F32, name="%s%d%d" % (kind, h, b), tag="bank%d" % bank)
            if kind == "logit":
                rhs, rhs_scale = l_codes[h][g][:].bitcast(FP8X4), l_plane[h][g][:]
            elif kind == "step":
                e_tile = e_first[g][:] if h == 0 else e_second[:, g, :]
                rhs, rhs_scale = e_tile.bitcast(FP4X4), e_plane[h][:, g, :]
            else:
                rhs, rhs_scale = f_codes[h][:, g, :].bitcast(FP8X4), f_plane[h][F_SCALE_ROW:P, g, :]
            x_tile = x_codes[g][:, tile_rows(b)] if b < HEAD else x_rest[:, g, tile_rows(b - HEAD)]
            nc.tensor.matmul_mx(
                out=live[kind, h, b][:],
                lhsT=x_tile.bitcast(FP8X4),
                lhsT_scale=x_plane[:, g, tile_rows(b)],
                rhs=rhs,
                rhs_scale=rhs_scale,
                start=(g == 0),
                stop=(g == PASSES - 1),
            )

        def plan_tile(h, b):
            return plan_sb[h][b // 3][:, b % 3, :]

        def sigmoid(h, b):
            live["gate", h, b] = sbuf("gate%d%d" % (h, b), [P, HALF], F32, tag="gate%d" % b)
            nc.scalar.activation(out=live["gate", h, b][:], in_=live["logit", h, b][:], func=SIGMOID)

        def gate_step(h, b):
            live["gated", h, b] = sbuf("gated%d%d" % (h, b), [P, HALF], F32, tag="gated%d" % b)
            nc.vector.tensor_tensor(
                out=live["gated", h, b][:], in0=live["step", h, b][:], in1=live["gate", h, b][:], op=MULT
            )

        def first_sum(engine, h, b):
            pair = (live["shift", h, b][:], live["gated", h, b][:]) if h == 0 else (live["gated", h, b][:], plan_tile(h, b))
            live["part", h, b] = sbuf("part%d%d" % (h, b), [P, HALF], F32, tag="part%d" % b)
            engine.tensor_tensor(out=live["part", h, b][:], in0=pair[0], in1=pair[1], op=ADD)

        def finish(engine, h, b):
            pair = (live["part", h, b][:], plan_tile(h, b)) if h == 0 else (live["shift", h, b][:], live["part", h, b][:])
            live["y", h, b] = sbuf("y%d%d" % (h, b), [P, HALF], F32)
            engine.tensor_tensor(out=live["y", h, b][:], in0=pair[0], in1=pair[1], op=ADD)

        def store_y(h, b):
            nc.sync.dma_start(out=out_0[tile_rows(b), cols(h)], in_=live["y", h, b][:])

        def round_y(h, b):
            live["y16", h, b] = sbuf("yr%d%d" % (h, b), [P, 2, P, 2], BF16, tag="yr%d" % b)
            src = live["y", h, b][:].rearrange("m (p u e) -> m u p e", u=2, e=2)
            nc.scalar.copy(out=live["y16", h, b][:], in_=src)

        def finish_rounded(h, b):
            live["y16", h, b] = sbuf("yr%d%d" % (h, b), [P, 2, P, 2], BF16, tag="yr%d" % b)
            nc.vector.tensor_tensor(
                out=live["y16", h, b][:],
                in0=live["shift", h, b][:].rearrange("m (p u e) -> m u p e", u=2, e=2),
                in1=live["part", h, b][:].rearrange("m (p u e) -> m u p e", u=2, e=2),
                op=ADD,
            )

        def turn(h, b0, count, bank):
            live["turned", h, b0] = psum.tile([P, count, 2, P], F32, name="turn%d%d" % (h, b0), tag="bank%d" % bank)
            for s in range(count):
                words = live["y16", h, b0 + s][:].rearrange("m u p e -> m (u p e)").bitcast(F32)
                for u in range(2):
                    nc.tensor.transpose(live["turned", h, b0][:, s, u, :], words[:, u * P : (u + 1) * P], ident[:])

        def regroup(engine, h, b0, count):
            live["yt", h, b0] = sbuf("yt%d%d" % (h, b0), [P, count * P * 4], BF16)
            dst = live["yt", h, b0][:].bitcast(F32).rearrange("p (s m u) -> p s m u", s=count, u=2)
            src = live["turned", h, b0][:].rearrange("p s u m -> p s m u")
            if engine == "vector":
                nc.vector.tensor_copy(out=dst, in_=src)
            else:
                nc.scalar.copy(out=dst, in_=src)

        def quantise_y(h, b0, count):
            m = slice(b0 * P, (b0 + count) * P)
            nc.vector.quantize_mx(out=y_codes[h][:, m].bitcast(FP8X4), scales=y_plane[h][:, m], in_=live["yt", h, b0][:])

        def store_codes(h, b0, count):
            m = slice(b0 * P, (b0 + count) * P)
            dst = out_1[h].rearrange("p m t -> p (m t)").bitcast(I32)[:, m]
            nc.sync.dma_start(out=dst, in_=y_codes[h][:, m].bitcast(I32))

        def store_scales(engine, h, quadrant):
            dst = out_2[h].bitcast(I32)[4 * quadrant : 4 * quadrant + 4, :]
            engine.dma_start(out=dst, in_=y_plane[h][32 * quadrant : 32 * quadrant + 4, :].bitcast(I32))

        queues = {"vector": [], "gpsimd": [], "sync": [], "scalar": [], "tensor": []}

        def put(queue, key, needs, call, *args):
            queues[queue].append((key, needs, call, args))

        bank_uses = []

        def take_bank(emptied_by):
            bank_uses.append(emptied_by)
            count = len(bank_uses) - 1
            return count % BANKS, ([bank_uses[count - BANKS]] if count >= BANKS else [])

        def emptier(kind, h, b):
            if kind == "logit":
                return ("sigmoid", h, b)
            if kind == "step":
                return ("gated", h, b)
            return ("part", h, b) if h == 0 else ("y", h, b)

        def operand_needs(kind, h, g):
            if kind == "logit":
                return [("ql", h, g)]
            if kind == "step":
                return [("e", h, g if h == 0 else 0), ("e_scales", h)]
            return [("f", h), ("f_scales", h)]

        def put_pass(kind, h, b, g, bank, waits):
            x_need = ("x", g) if b < HEAD else "x_rest"
            put("tensor", (kind, h, b, g), [x_need, "x_scales"] + operand_needs(kind, h, g) + waits,
                product_pass, kind, h, b, g, bank)

        def put_product(kind, h, b):
            bank, waits = take_bank(emptier(kind, h, b))
            for g in passes:
                put_pass(kind, h, b, g, bank, waits)

        def group_of(h, b):
            return [(h, b0) for (hh, b0, count) in GROUPS if hh == h and b0 <= b < b0 + count][0]

        def put_token(queue, token):
            op, h, b = token[0], int(token[1]), int(token[2])
            engine = {"vector": nc.vector, "gpsimd": nc.gpsimd, "scalar": nc.scalar, "sync": nc.sync, "tensor": nc.tensor}[queue]
            count = ([c for (hh, b0, c) in GROUPS if (hh, b0) == (h, b)] + [0])[0]
            if op in "LSF":
                put_product({"L": "logit", "S": "step", "F": "shift"}[op], h, b)
            elif op == "T":
                bank, waits = take_bank(("yt", h, b))
                put(queue, ("turned", h, b), [("y16", h, b + s) for s in range(count)] + ["ident"] + waits,
                    turn, h, b, count, bank)
            elif op == "g":
                put(queue, ("gated", h, b), [("step", h, b, 2), ("sigmoid", h, b)] + ([("part", 0, b)] if h else []),
                    gate_step, h, b)
            elif op == "p":
                other = [("shift", h, b, 2)] if h == 0 else [("plan", h, b // 3), ("y", 0, b)]
                put(queue, ("part", h, b), [("gated", h, b)] + other, first_sum, engine, h, b)
            elif op == "y":
                last = ("plan", h, b // 3) if h == 0 else ("shift", h, b, 2)
                put(queue, ("y", h, b), [last, ("part", h, b)], finish, engine, h, b)
            elif op == "r":
                put(queue, ("y16", h, b), [("shift", h, b, 2), ("part", h, b), ("turned",) + group_of(0, b)], finish_rounded, h, b)
            elif op == "Q":
                put(queue, ("ql", h, b), [("il", h, b, "scalar"), ("il", h, b, "vector")], quantise_l, h, b)
            elif op == "I":
                put(queue, ("il", h, b, queue), [("l", h, b)], interleave, queue, h, b)
            elif op == "q":
                put(queue, ("qy", h, b), [("yt", h, b)], quantise_y, h, b, count)
            elif op == "s":
                put(queue, ("sigmoid", h, b), [("logit", h, b, 2)] + ([("gated", 0, b)] if h else []), sigmoid, h, b)
            elif op == "c":
                put(queue, ("y16", h, b), [("y", h, b)] + ([("turned",) + group_of(0, b)] if h else []), round_y, h, b)
            elif op == "R":
                put(queue, ("yt", h, b), [("turned", h, b)], regroup, queue, h, b, count)
            elif op == "Y":
                put(queue, ("store_y", h, b), [("y", h, b)], store_y, h, b)
            elif op == "W":
                put(queue, ("codes", h, b), [("qy", h, b)], store_codes, h, b, count)
            elif op == "w":
                put(queue, ("codes", h, b), [("qy", h, b0) for (hh, b0, c) in GROUPS if hh == h and b0 >= b],
                    store_codes, h, b, ROW_TILES - b)
            elif op == "Z":
                put(queue, ("scales", h, b), [("qy", hh, b0) for (hh, b0, c) in GROUPS if hh == h], store_scales, engine, h, b)
            elif op == "l":
                put(queue, ("l", h, b), [], load_l, h, b)
            elif op == "x":
                put(queue, ("x", b), [], load_x, b)
            elif op == "X":
                put(queue, "x_rest", [], load_x_rest)
            elif op == "e":
                put(queue, ("e", h, b), [], load_e, h, b)
            elif op == "f":
                put(queue, ("f", h), [], load_f, h)
            elif op == "P":
                put(queue, ("plan", h, b), [], load_plan, h, b)
            elif op == "j":
                put(queue, ("f_scales", h), [("clear_f", h)], load_scales, f_plane[h], f_scales[:, :, cols(h)], F_SCALE_ROW)
            elif op == "i":
                put(queue, ("e_scales", h), [("clear_e", h)], load_scales, e_plane[h], e_scales[:, :, cols(h)], 0)
            elif op == "v":
                put(queue, ("codes", h, b), [("qy", h, b0) for (hh, b0, c) in GROUPS if hh == h and b <= b0 < 5],
                    store_codes, h, b, 5 - b)
            else:
                put(queue, "x_scales", ["clear_x"], load_scales, x_plane, x_scales, 0)

        put("vector", "warm_in", [], nc.vector.memset, warm_in[:], 0.0)
        put("vector", "clear_x", [], clear, x_plane)
        put("vector", "ones", [], nc.vector.memset, ones[:], 1.0)
        put("vector", ("clear_e", 0), [], clear, e_plane[0])
        put("vector", "ones_codes", [], nc.vector.quantize_mx, ones_codes[:].bitcast(FP8X4), ones_plane[:], ones[:])
        put("vector", ("clear_f", 0), [], clear, f_plane[0])
        put("vector", ("clear_e", 1), [], clear, e_plane[1])
        put("vector", ("clear_f", 1), [], clear, f_plane[1])
        put("tensor", "warm_tensor", ["ones_codes"], warm_tensor)
        put("gpsimd", "ident", [], make_identity, nc, ident[:])
        put("scalar", "warm", ["warm_in"], nc.scalar.activation, warm[:], warm_in[:], SIGMOID)

        head_banks = {(kind, b): take_bank(emptier(kind, 0, b))[0] for kind in ("logit", "step") for b in range(HEAD)}
        for kind, g in HEAD_ORDER:
            for b in range(HEAD):
                put_pass(kind, 0, b, g, head_banks[kind, b], [])

        for queue, order in (("tensor", TENSOR), ("vector", VECTOR), ("scalar", SCALAR), ("gpsimd", GPSIMD), ("sync", SYNC)):
            for token in order.split():
                put_token(queue, token)

        written = set()
        heads = {name: 0 for name in queues}
        total = sum(len(q) for q in queues.values())
        while len(written) < total:
            before = len(written)
            for name, queue in queues.items():
                while heads[name] < len(queue) and all(need in written for need in queue[heads[name]][1]):
                    key, needs, call, args = queue[heads[name]]
                    call(*args)
                    written.add(key)
                    heads[name] += 1
            assert len(written) > before, [queues[n][heads[n]][:2] for n in queues if heads[n] < len(queues[n])]
